import numpy as np
import ml_dtypes

BF16 = ml_dtypes.bfloat16


def bf(x):
    return np.asarray(x, np.float32).astype(BF16)


def f32(x):
    return np.asarray(x, np.float32)


def f64(x):
    return np.asarray(x).astype(np.float64)


def striped(idx):
    return np.tile(idx.reshape(-1, 16).T, (8, 1))


def rows(idx, k):
    return np.tile(idx, (k, 1))


def look(tab, idx):
    return np.take_along_axis(f64(tab), rows(idx, len(tab)), axis=1)


K, S, D, V, N = 512, 2048, 2, 1024, 2048


def setup_inputs():
    return {"tab": f32(np.random.standard_normal((K, S))), "x0": f32(1.0 * np.random.standard_normal((K, V))), "offs": striped(np.random.permutation(S)[:N])}


def reference(tab, x0, offs):
    idx = offs[:16].T.reshape(-1)
    m = f64(x0)
    for d in range(D):
        m = np.maximum(m, look(tab, idx[d * V:(d + 1) * V]))
    x = m + np.log(np.exp(f64(x0) - m) + sum(np.exp(look(tab, idx[d * V:(d + 1) * V]) - m) for d in range(D)))
    return x

@@ -1,0 +1,65 @@
+import concourse.mybir as mybir
+from concourse.masks import make_identity
+
+P = 128
+S = 2048
+V = 1024
+D = 2
+N = D * V
+BANK = 512
+F32 = mybir.dt.float32
+U16 = mybir.dt.uint16
+MAX = mybir.AluOpType.max
+SUB = mybir.AluOpType.subtract
+ADD = mybir.AluOpType.add
+EXP = mybir.ActivationFunctionType.Exp
+LN = mybir.ActivationFunctionType.Ln
+
+
+def tile_lookup_lse_out_kernel(tc, tab, x0, offs, out):
+    nc = tc.nc
+    with (
+        tc.tile_pool(name="held", bufs=1) as held,
+        tc.tile_pool(name="loads", bufs=4) as loads,
+        tc.tile_pool(name="work", bufs=2) as work,
+        tc.psum_pool(name="psum", bufs=4) as psum,
+    ):
+        offsets = held.tile([P, N // 16], U16, name="offsets")
+        nc.sync.dma_start(offsets[:], offs)
+        identity = held.tile([P, P], F32, name="identity")
+        make_identity(nc, identity[:])
+
+        for b in range(tab.shape[0] // P):
+            rows = slice(b * P, (b + 1) * P)
+            window = loads.tile([P, S], F32, name="window")
+            nc.sync.dma_start(window[:], tab[rows, :])
+            node = loads.tile([P, V], F32, name="node")
+            nc.sync.dma_start(node[:], x0[rows, :])
+
+            picked = [window[:].indirect(offsets[:, n * V // 16 : (n + 1) * V // 16]) for n in range(D)]
+
+            first = work.tile([P, V], F32, name="first")
+            nc.vector.tensor_tensor(first[:], picked[0], node[:], MAX)
+            highest = work.tile([P, V], F32, name="highest")
+            nc.vector.tensor_tensor(highest[:], picked[1], first[:], MAX)
+
+            below = work.tile([P, D + 1, V], F32, name="below")
+            nc.vector.tensor_tensor(below[:, 0, :], node[:], highest[:], SUB)
+            for n in range(D):
+                nc.vector.tensor_tensor(below[:, n + 1, :], picked[n], highest[:], SUB)
+
+            weight = work.tile([P, D + 1, V], F32, name="weight")
+            for k in range(D + 1):
+                nc.scalar.activation(weight[:, k, :], below[:, k, :], EXP)
+
+            logs = work.tile([P, V], F32, name="logs")
+            for c in range(V // BANK):
+                cols = slice(c * BANK, (c + 1) * BANK)
+                total = psum.tile([P, BANK], F32, name="total")
+                for k in range(D + 1):
+                    nc.tensor.matmul(total[:], identity[:], weight[:, k, cols], start=(k == 0), stop=(k == D))
+                nc.scalar.activation(logs[:, cols], total[:], LN)
+
+            result = work.tile([P, V], F32, name="result")
+            nc.vector.tensor_tensor(result[:], logs[:], highest[:], ADD)
+            nc.sync.dma_start(out[rows, :], result[:])

@@ -18,9 +18,11 @@ LN = mybir.ActivationFunctionType.Ln
 
 def tile_lookup_lse_out_kernel(tc, tab, x0, offs, out):
     nc = tc.nc
+    blocks = tab.shape[0] // P
+    pieces = [slice(c, c + BANK) for c in range(0, V, BANK)]
     with (
         tc.tile_pool(name="held", bufs=1) as held,
-        tc.tile_pool(name="loads", bufs=4) as loads,
+        tc.tile_pool(name="loads", bufs=blocks) as loads,
         tc.tile_pool(name="work", bufs=2) as work,
         tc.psum_pool(name="psum", bufs=4) as psum,
     ):
@@ -29,37 +31,46 @@ def tile_lookup_lse_out_kernel(tc, tab, x0, offs, out):
         identity = held.tile([P, P], F32, name="identity")
         make_identity(nc, identity[:])
 
-        for b in range(tab.shape[0] // P):
+        def picked(window, n, cols):
+            start, stop = (n * V + cols.start) // 16, (n * V + cols.stop) // 16
+            return window[:].indirect(offsets[:, start:stop])
+
+        def sums(b):
             rows = slice(b * P, (b + 1) * P)
             window = loads.tile([P, S], F32, name="window")
-            nc.sync.dma_start(window[:], tab[rows, :])
+            (nc.scalar if b == 0 else nc.sync).dma_start(window[:], tab[rows, :])
             node = loads.tile([P, V], F32, name="node")
             nc.sync.dma_start(node[:], x0[rows, :])
 
-            picked = [window[:].indirect(offsets[:, n * V // 16 : (n + 1) * V // 16]) for n in range(D)]
-
             first = work.tile([P, V], F32, name="first")
-            nc.vector.tensor_tensor(first[:], picked[0], node[:], MAX)
             highest = work.tile([P, V], F32, name="highest")
-            nc.vector.tensor_tensor(highest[:], picked[1], first[:], MAX)
+            for cols in pieces:
+                nc.vector.tensor_tensor(first[:, cols], picked(window, 0, cols), node[:, cols], MAX)
+            for cols in pieces:
+                nc.vector.tensor_tensor(highest[:, cols], picked(window, 1, cols), first[:, cols], MAX)
 
-            below = work.tile([P, D + 1, V], F32, name="below")
-            nc.vector.tensor_tensor(below[:, 0, :], node[:], highest[:], SUB)
-            for n in range(D):
-                nc.vector.tensor_tensor(below[:, n + 1, :], picked[n], highest[:], SUB)
-
-            weight = work.tile([P, D + 1, V], F32, name="weight")
+            totals = [psum.tile([P, BANK], F32, name="total") for cols in pieces]
             for k in range(D + 1):
-                nc.scalar.activation(weight[:, k, :], below[:, k, :], EXP)
+                below = work.tile([P, V], F32, name=f"below{k}")
+                weight = work.tile([P, V], F32, name=f"weight{k}")
+                for cols, total in zip(pieces, totals):
+                    other = node[:, cols] if k == 0 else picked(window, k - 1, cols)
+                    nc.vector.tensor_tensor(below[:, cols], other, highest[:, cols], SUB)
+                    nc.scalar.activation(weight[:, cols], below[:, cols], EXP)
+                    nc.tensor.matmul(total[:], identity[:], weight[:, cols], start=(k == 0), stop=(k == D))
+            return rows, highest, totals
 
+        def finish(rows, highest, totals):
             logs = work.tile([P, V], F32, name="logs")
-            for c in range(V // BANK):
-                cols = slice(c * BANK, (c + 1) * BANK)
-                total = psum.tile([P, BANK], F32, name="total")
-                for k in range(D + 1):
-                    nc.tensor.matmul(total[:], identity[:], weight[:, k, cols], start=(k == 0), stop=(k == D))
-                nc.scalar.activation(logs[:, cols], total[:], LN)
-
             result = work.tile([P, V], F32, name="result")
-            nc.vector.tensor_tensor(result[:], logs[:], highest[:], ADD)
-            nc.sync.dma_start(out[rows, :], result[:])
+            for cols, total in zip(pieces, totals):
+                nc.scalar.activation(logs[:, cols], total[:], LN)
+                nc.vector.tensor_tensor(result[:, cols], logs[:, cols], highest[:, cols], ADD)
+                nc.sync.dma_start(out[rows, cols], result[:, cols])
+
+        waiting = sums(0)
+        for b in range(1, blocks):
+            summed = sums(b)
+            finish(*waiting)
+            waiting = summed
+        finish(*waiting)

@@ -19,11 +19,11 @@ LN = mybir.ActivationFunctionType.Ln
 def tile_lookup_lse_out_kernel(tc, tab, x0, offs, out):
     nc = tc.nc
     blocks = tab.shape[0] // P
-    pieces = [slice(c, c + BANK) for c in range(0, V, BANK)]
+    halves = [slice(c, c + BANK) for c in range(0, V, BANK)]
     with (
         tc.tile_pool(name="held", bufs=1) as held,
         tc.tile_pool(name="loads", bufs=blocks) as loads,
-        tc.tile_pool(name="work", bufs=2) as work,
+        tc.tile_pool(name="work", bufs=3) as work,
         tc.psum_pool(name="psum", bufs=4) as psum,
     ):
         offsets = held.tile([P, N // 16], U16, name="offsets")
@@ -31,46 +31,57 @@ def tile_lookup_lse_out_kernel(tc, tab, x0, offs, out):
         identity = held.tile([P, P], F32, name="identity")
         make_identity(nc, identity[:])
 
-        def picked(window, n, cols):
-            start, stop = (n * V + cols.start) // 16, (n * V + cols.stop) // 16
-            return window[:].indirect(offsets[:, start:stop])
-
-        def sums(b):
+        pieces = [halves if b in (0, blocks - 1) else [slice(0, V)] for b in range(blocks)]
+        windows, nodes = [], []
+        for b in range(blocks):
             rows = slice(b * P, (b + 1) * P)
             window = loads.tile([P, S], F32, name="window")
-            (nc.scalar if b == 0 else nc.sync).dma_start(window[:], tab[rows, :])
+            nc.sync.dma_start(window[:], tab[rows, :])
             node = loads.tile([P, V], F32, name="node")
-            nc.sync.dma_start(node[:], x0[rows, :])
+            for cols in pieces[b]:
+                nc.sync.dma_start(node[:, cols], x0[rows, cols])
+            windows.append(window)
+            nodes.append(node)
 
-            first = work.tile([P, V], F32, name="first")
-            highest = work.tile([P, V], F32, name="highest")
-            for cols in pieces:
-                nc.vector.tensor_tensor(first[:, cols], picked(window, 0, cols), node[:, cols], MAX)
-            for cols in pieces:
-                nc.vector.tensor_tensor(highest[:, cols], picked(window, 1, cols), first[:, cols], MAX)
+        def picked(b, n, cols):
+            start, stop = (n * V + cols.start) // 16, (n * V + cols.stop) // 16
+            return windows[b][:].indirect(offsets[:, start:stop])
 
-            totals = [psum.tile([P, BANK], F32, name="total") for cols in pieces]
+        def maximum(b, n, previous):
+            larger = work.tile([P, V], F32, name=f"larger{n}")
+            for cols in pieces[b]:
+                nc.vector.tensor_tensor(larger[:, cols], picked(b, n, cols), previous[:, cols], MAX)
+            return larger
+
+        def exponentials(b, highest):
+            totals = [psum.tile([P, BANK], F32, name="total") for cols in halves]
             for k in range(D + 1):
                 below = work.tile([P, V], F32, name=f"below{k}")
                 weight = work.tile([P, V], F32, name=f"weight{k}")
-                for cols, total in zip(pieces, totals):
-                    other = node[:, cols] if k == 0 else picked(window, k - 1, cols)
-                    nc.vector.tensor_tensor(below[:, cols], other, highest[:, cols], SUB)
+                for cols in pieces[b]:
+                    value = nodes[b][:, cols] if k == 0 else picked(b, k - 1, cols)
+                    nc.vector.tensor_tensor(below[:, cols], value, highest[:, cols], SUB)
                     nc.scalar.activation(weight[:, cols], below[:, cols], EXP)
+                for cols, total in zip(halves, totals):
                     nc.tensor.matmul(total[:], identity[:], weight[:, cols], start=(k == 0), stop=(k == D))
-            return rows, highest, totals
+            return totals
 
-        def finish(rows, highest, totals):
+        def finish(b, highest, totals):
             logs = work.tile([P, V], F32, name="logs")
             result = work.tile([P, V], F32, name="result")
-            for cols, total in zip(pieces, totals):
+            for cols, total in zip(halves, totals):
                 nc.scalar.activation(logs[:, cols], total[:], LN)
                 nc.vector.tensor_tensor(result[:, cols], logs[:, cols], highest[:, cols], ADD)
-                nc.sync.dma_start(out[rows, cols], result[:, cols])
+                nc.sync.dma_start(out[b * P : (b + 1) * P, cols], result[:, cols])
 
-        waiting = sums(0)
-        for b in range(1, blocks):
-            summed = sums(b)
-            finish(*waiting)
-            waiting = summed
+        first = maximum(0, 0, nodes[0])
+        waiting = None
+        for b in range(blocks):
+            highest = maximum(b, 1, first)
+            if b + 1 < blocks:
+                first = maximum(b + 1, 0, nodes[b + 1])
+            totals = exponentials(b, highest)
+            if waiting:
+                finish(*waiting)
+            waiting = (b, highest, totals)
         finish(*waiting)

@@ -20,25 +20,27 @@ def tile_lookup_lse_out_kernel(tc, tab, x0, offs, out):
     nc = tc.nc
     blocks = tab.shape[0] // P
     halves = [slice(c, c + BANK) for c in range(0, V, BANK)]
+    shrinking = [slice(0, BANK), slice(BANK, BANK + BANK // 2), slice(BANK + BANK // 2, V)]
     with (
         tc.tile_pool(name="held", bufs=1) as held,
         tc.tile_pool(name="loads", bufs=blocks) as loads,
         tc.tile_pool(name="work", bufs=3) as work,
-        tc.psum_pool(name="psum", bufs=4) as psum,
+        tc.psum_pool(name="psum", bufs=8) as psum,
     ):
         offsets = held.tile([P, N // 16], U16, name="offsets")
         nc.sync.dma_start(offsets[:], offs)
         identity = held.tile([P, P], F32, name="identity")
         make_identity(nc, identity[:])
 
-        pieces = [halves if b in (0, blocks - 1) else [slice(0, V)] for b in range(blocks)]
+        pieces = [halves] + [[slice(0, V)]] * (blocks - 2) + [shrinking]
+        banks = [halves] * (blocks - 1) + [shrinking]
         windows, nodes = [], []
         for b in range(blocks):
             rows = slice(b * P, (b + 1) * P)
             window = loads.tile([P, S], F32, name="window")
             nc.sync.dma_start(window[:], tab[rows, :])
             node = loads.tile([P, V], F32, name="node")
-            for cols in pieces[b]:
+            for cols in (halves if b == 0 else [slice(0, V)]):
                 nc.sync.dma_start(node[:, cols], x0[rows, cols])
             windows.append(window)
             nodes.append(node)
@@ -54,7 +56,7 @@ def tile_lookup_lse_out_kernel(tc, tab, x0, offs, out):
             return larger
 
         def exponentials(b, highest):
-            totals = [psum.tile([P, BANK], F32, name="total") for cols in halves]
+            totals = [psum.tile([P, cols.stop - cols.start], F32, name="total") for cols in banks[b]]
             for k in range(D + 1):
                 below = work.tile([P, V], F32, name=f"below{k}")
                 weight = work.tile([P, V], F32, name=f"weight{k}")
@@ -62,14 +64,14 @@ def tile_lookup_lse_out_kernel(tc, tab, x0, offs, out):
                     value = nodes[b][:, cols] if k == 0 else picked(b, k - 1, cols)
                     nc.vector.tensor_tensor(below[:, cols], value, highest[:, cols], SUB)
                     nc.scalar.activation(weight[:, cols], below[:, cols], EXP)
-                for cols, total in zip(halves, totals):
+                for cols, total in zip(banks[b], totals):
                     nc.tensor.matmul(total[:], identity[:], weight[:, cols], start=(k == 0), stop=(k == D))
             return totals
 
         def finish(b, highest, totals):
             logs = work.tile([P, V], F32, name="logs")
             result = work.tile([P, V], F32, name="result")
-            for cols, total in zip(halves, totals):
+            for cols, total in zip(banks[b], totals):
                 nc.scalar.activation(logs[:, cols], total[:], LN)
                 nc.vector.tensor_tensor(result[:, cols], logs[:, cols], highest[:, cols], ADD)
                 nc.sync.dma_start(out[b * P : (b + 1) * P, cols], result[:, cols])

@@ -19,28 +19,26 @@ LN = mybir.ActivationFunctionType.Ln
 def tile_lookup_lse_out_kernel(tc, tab, x0, offs, out):
     nc = tc.nc
     blocks = tab.shape[0] // P
+    whole = [slice(0, V)]
     halves = [slice(c, c + BANK) for c in range(0, V, BANK)]
-    shrinking = [slice(0, BANK), slice(BANK, BANK + BANK // 2), slice(BANK + BANK // 2, V)]
     with (
         tc.tile_pool(name="held", bufs=1) as held,
-        tc.tile_pool(name="loads", bufs=blocks) as loads,
-        tc.tile_pool(name="work", bufs=3) as work,
-        tc.psum_pool(name="psum", bufs=8) as psum,
+        tc.tile_pool(name="rows", bufs=blocks) as each,
+        tc.tile_pool(name="work", bufs=2) as work,
+        tc.psum_pool(name="psum", bufs=4) as psum,
     ):
         offsets = held.tile([P, N // 16], U16, name="offsets")
         nc.sync.dma_start(offsets[:], offs)
         identity = held.tile([P, P], F32, name="identity")
         make_identity(nc, identity[:])
 
-        pieces = [halves] + [[slice(0, V)]] * (blocks - 2) + [shrinking]
-        banks = [halves] * (blocks - 1) + [shrinking]
         windows, nodes = [], []
         for b in range(blocks):
             rows = slice(b * P, (b + 1) * P)
-            window = loads.tile([P, S], F32, name="window")
+            window = each.tile([P, S], F32, name="window")
             nc.sync.dma_start(window[:], tab[rows, :])
-            node = loads.tile([P, V], F32, name="node")
-            for cols in (halves if b == 0 else [slice(0, V)]):
+            node = each.tile([P, V], F32, name="node")
+            for cols in halves if b == 0 else whole:
                 nc.sync.dma_start(node[:, cols], x0[rows, cols])
             windows.append(window)
             nodes.append(node)
@@ -49,41 +47,42 @@ def tile_lookup_lse_out_kernel(tc, tab, x0, offs, out):
             start, stop = (n * V + cols.start) // 16, (n * V + cols.stop) // 16
             return windows[b][:].indirect(offsets[:, start:stop])
 
-        def maximum(b, n, previous):
-            larger = work.tile([P, V], F32, name=f"larger{n}")
-            for cols in pieces[b]:
+        def maximum(b, n, previous, pieces):
+            larger = each.tile([P, V], F32, name=f"larger{n}")
+            for cols in pieces:
                 nc.vector.tensor_tensor(larger[:, cols], picked(b, n, cols), previous[:, cols], MAX)
             return larger
 
-        def exponentials(b, highest):
-            totals = [psum.tile([P, cols.stop - cols.start], F32, name="total") for cols in banks[b]]
+        def logarithm(b, highest):
+            totals = [psum.tile([P, cols.stop - cols.start], F32, name="total") for cols in halves]
             for k in range(D + 1):
                 below = work.tile([P, V], F32, name=f"below{k}")
                 weight = work.tile([P, V], F32, name=f"weight{k}")
-                for cols in pieces[b]:
+                for cols in halves if b == blocks - 1 and k == D else whole:
                     value = nodes[b][:, cols] if k == 0 else picked(b, k - 1, cols)
                     nc.vector.tensor_tensor(below[:, cols], value, highest[:, cols], SUB)
                     nc.scalar.activation(weight[:, cols], below[:, cols], EXP)
-                for cols, total in zip(banks[b], totals):
+                for cols, total in zip(halves, totals):
                     nc.tensor.matmul(total[:], identity[:], weight[:, cols], start=(k == 0), stop=(k == D))
-            return totals
-
-        def finish(b, highest, totals):
-            logs = work.tile([P, V], F32, name="logs")
-            result = work.tile([P, V], F32, name="result")
-            for cols, total in zip(banks[b], totals):
+            logs = each.tile([P, V], F32, name="logs")
+            for cols, total in zip(halves, totals):
                 nc.scalar.activation(logs[:, cols], total[:], LN)
+            return logs
+
+        def finish(b, highest, logs, pieces):
+            result = work.tile([P, V], F32, name="result")
+            for cols in pieces:
                 nc.vector.tensor_tensor(result[:, cols], logs[:, cols], highest[:, cols], ADD)
                 nc.sync.dma_start(out[b * P : (b + 1) * P, cols], result[:, cols])
 
-        first = maximum(0, 0, nodes[0])
-        waiting = None
+        first = maximum(0, 0, nodes[0], halves)
+        highest, logs = [], []
         for b in range(blocks):
-            highest = maximum(b, 1, first)
+            highest.append(maximum(b, 1, first, halves if b == 0 else whole))
             if b + 1 < blocks:
-                first = maximum(b + 1, 0, nodes[b + 1])
-            totals = exponentials(b, highest)
-            if waiting:
-                finish(*waiting)
-            waiting = (b, highest, totals)
-        finish(*waiting)
+                first = maximum(b + 1, 0, nodes[b + 1], whole)
+            else:
+                finish(0, highest[0], logs[0], whole)
+            logs.append(logarithm(b, highest[b]))
+        for b in range(1, blocks):
+            finish(b, highest[b], logs[b], halves if b == blocks - 1 else whole)

import concourse.mybir as mybir
from concourse.masks import make_identity

P = 128
S = 2048
V = 1024
D = 2
N = D * V
BANK = 512
F32 = mybir.dt.float32
U16 = mybir.dt.uint16
MAX = mybir.AluOpType.max
SUB = mybir.AluOpType.subtract
ADD = mybir.AluOpType.add
EXP = mybir.ActivationFunctionType.Exp
LN = mybir.ActivationFunctionType.Ln


def tile_lookup_lse_out_kernel(tc, tab, x0, offs, out):
    nc = tc.nc
    blocks = tab.shape[0] // P
    whole = [slice(0, V)]
    halves = [slice(c, c + BANK) for c in range(0, V, BANK)]
    with (
        tc.tile_pool(name="held", bufs=1) as held,
        tc.tile_pool(name="rows", bufs=blocks) as each,
        tc.tile_pool(name="work", bufs=2) as work,
        tc.psum_pool(name="psum", bufs=4) as psum,
    ):
        offsets = held.tile([P, N // 16], U16, name="offsets")
        nc.sync.dma_start(offsets[:], offs)
        identity = held.tile([P, P], F32, name="identity")
        make_identity(nc, identity[:])

        windows, nodes = [], []
        for b in range(blocks):
            rows = slice(b * P, (b + 1) * P)
            window = each.tile([P, S], F32, name="window")
            nc.sync.dma_start(window[:], tab[rows, :])
            node = each.tile([P, V], F32, name="node")
            for cols in halves if b == 0 else whole:
                nc.sync.dma_start(node[:, cols], x0[rows, cols])
            windows.append(window)
            nodes.append(node)

        def picked(b, n, cols):
            start, stop = (n * V + cols.start) // 16, (n * V + cols.stop) // 16
            return windows[b][:].indirect(offsets[:, start:stop])

        def maximum(b, n, previous, pieces):
            larger = each.tile([P, V], F32, name=f"larger{n}")
            for cols in pieces:
                nc.vector.tensor_tensor(larger[:, cols], picked(b, n, cols), previous[:, cols], MAX)
            return larger

        def logarithm(b, highest):
            totals = [psum.tile([P, cols.stop - cols.start], F32, name="total") for cols in halves]
            for k in range(D + 1):
                below = work.tile([P, V], F32, name=f"below{k}")
                weight = work.tile([P, V], F32, name=f"weight{k}")
                for cols in halves if b == blocks - 1 and k == D else whole:
                    value = nodes[b][:, cols] if k == 0 else picked(b, k - 1, cols)
                    nc.vector.tensor_tensor(below[:, cols], value, highest[:, cols], SUB)
                    nc.scalar.activation(weight[:, cols], below[:, cols], EXP)
                for cols, total in zip(halves, totals):
                    nc.tensor.matmul(total[:], identity[:], weight[:, cols], start=(k == 0), stop=(k == D))
            logs = each.tile([P, V], F32, name="logs")
            for cols, total in zip(halves, totals):
                nc.scalar.activation(logs[:, cols], total[:], LN)
            return logs

        def finish(b, highest, logs, pieces):
            result = work.tile([P, V], F32, name="result")
            for cols in pieces:
                nc.vector.tensor_tensor(result[:, cols], logs[:, cols], highest[:, cols], ADD)
                nc.sync.dma_start(out[b * P : (b + 1) * P, cols], result[:, cols])

        first = maximum(0, 0, nodes[0], halves)
        highest, logs = [], []
        for b in range(blocks):
            highest.append(maximum(b, 1, first, halves if b == 0 else whole))
            if b + 1 < blocks:
                first = maximum(b + 1, 0, nodes[b + 1], whole)
            else:
                finish(0, highest[0], logs[0], whole)
            logs.append(logarithm(b, highest[b]))
        for b in range(1, blocks):
            finish(b, highest[b], logs[b], halves if b == blocks - 1 else whole)
